import numpy as np
import ml_dtypes


def mxq(x, axis, fmt="e4m3"):
    dtype, down = {"e4m3": (ml_dtypes.float8_e4m3fn, 7), "e5m2": (ml_dtypes.float8_e5m2, 14)}[fmt]
    v = np.moveaxis(np.asarray(x, np.float32).astype(ml_dtypes.bfloat16).astype(np.float64), axis, -1)
    blocks = v.reshape(v.shape[:-1] + (-1, 32))
    amax = np.abs(blocks).max(-1, keepdims=True)
    byte = np.maximum(np.where(amax > 0, np.frexp(amax)[1] - 1 + 127, 0) - down, 1)
    scale = np.exp2(byte - 127.0)
    codes = (blocks / scale).astype(np.float32).astype(dtype).astype(np.float64)
    return np.moveaxis((codes * scale).reshape(v.shape), -1, axis)


WIDE = False


def mx_kscale(k):
    if not WIDE:
        return np.ones(k)
    levels = np.array([10, -10, 5, -5, 0])
    if k % 512:
        return np.exp2(np.random.permutation(np.resize(levels, k // 32))).repeat(32)
    a = np.empty((k // 512, 16))
    for p in range(k // 512):
        a[p, :8] = np.random.permutation(np.resize(levels, 8))
        for g in range(8):
            far = levels[np.abs(levels - a[p, g]) >= 10]
            a[p, g + 8] = far[np.random.randint(len(far))]
    return np.exp2(a.ravel()).repeat(32)


def f64(x):
    return np.asarray(x).astype(np.float64)


def striped8(idx):
    return np.asarray(idx).reshape(8, -1, 16).transpose(0, 2, 1).reshape(128, -1).astype(np.uint16)


def unstriped8(offs):
    return offs.reshape(8, 16, -1).transpose(0, 2, 1).reshape(8, -1).astype(np.int64)


def pick8(x, idx, run):
    r = np.arange(len(x))
    return x[r[:, None], idx[r % (8 * run) // run]]


E2M1 = np.array([0.0, 0.5, 1.0, 1.5, 2.0, 3.0, 4.0, 6.0, -0.0, -0.5, -1.0, -1.5, -2.0, -3.0, -4.0, -6.0])


def pack_weight(w, fmt):
    k, n = w.shape
    w = f64(np.asarray(w, np.float32).astype(ml_dtypes.bfloat16)).reshape(k // 32, 32, n)
    amax = np.abs(w).max(1)
    if fmt == "e4m3":
        byte = np.frexp(amax)[1] - 1 + 127 - 7
    else:
        mant, ex = np.frexp(amax / 6.0)
        byte = np.where(mant > 0.5, ex, ex - 1) + 127
    byte = np.clip(np.where(amax > 0, byte, 1), 1, 254)
    scaled = (w * np.exp2(127.0 - byte)[:, None, :]).reshape(k, n).astype(np.float32)
    by_word = np.ascontiguousarray(scaled.reshape(k // 512, 128, 4, n).transpose(0, 1, 3, 2))
    if fmt == "e4m3":
        words = by_word.astype(ml_dtypes.float8_e4m3fn).view(np.uint8)
    else:
        c = by_word.astype(ml_dtypes.float4_e2m1fn).view(np.uint8) & 0xF
        words = (c[..., 0::2] | (c[..., 1::2] << 4)).reshape(k // 512, 128, 2 * n)
    return np.ascontiguousarray(words), np.ascontiguousarray(byte.astype(np.uint8).reshape(k // 512, 16, n))


def unpack_weight(words, scales, fmt):
    g, _, n = scales.shape
    words = np.ascontiguousarray(words).reshape(g, 128, n, -1)
    if fmt == "e4m3":
        vals = words.view(ml_dtypes.float8_e4m3fn).astype(np.float64)
    else:
        nib = np.empty((g, 128, n, 4), np.uint8)
        nib[..., 0::2] = words & 0xF
        nib[..., 1::2] = words >> 4
        vals = E2M1[nib]
    vals = vals * np.repeat(np.exp2(scales.astype(np.float64) - 127.0), 8, axis=1)[..., None]
    return vals.transpose(0, 1, 3, 2).reshape(g * 512, n)


K, L, S, T, N = 1024, 512, 512, 512, 512


def setup_inputs():
    n = np.random.standard_normal
    idx = np.stack([np.random.randint(0, S, T) for _ in range(8)])
    idx2 = np.stack([np.random.randint(0, S, T) for _ in range(8)])
    fk = mx_kscale(K)
    fl = mx_kscale(L)
    xap = pack_weight(n((K, S)) / fk[:, None], "e4m3")
    xbp = pack_weight(n((L, S)) / fl[:, None], "e2m1")
    wbp = pack_weight(n((L, N)) * 1 / np.sqrt(L) * fl[:, None], "e4m3")
    return {
        "xa_words": xap[0],
        "xa_scales": xap[1],
        "wa": (n((K, N)) * 1 / np.sqrt(K) * fk[:, None]).astype(np.float32),
        "xb_words": xbp[0],
        "xb_scales": xbp[1],
        "wb_words": wbp[0],
        "wb_scales": wbp[1],
        "ga": (np.random.uniform(0.3, 1.0, (1, T))).astype(np.float32),
        "gb": (np.random.uniform(0.3, 1.0, (1, T))).astype(np.float32),
        "offs": striped8(idx),
        "offs2": striped8(idx2),
    }


def reference(xa_words, xa_scales, wa, xb_words, xb_scales, wb_words, wb_scales, ga, gb, offs, offs2):
    idx = unstriped8(offs)
    idx2 = unstriped8(offs2)
    xau = unpack_weight(xa_words, xa_scales, "e4m3")
    xbu = unpack_weight(xb_words, xb_scales, "e2m1")
    wbu = unpack_weight(wb_words, wb_scales, "e4m3")
    waq = mxq(f64(wa), 0, "e4m3")
    za = waq.T @ xau
    zb = wbu.T @ xbu
    y = f64(ga) * pick8(za, idx, 64) + f64(gb) * pick8(zb, idx2, 64)
    return y

@@ -1,0 +1,189 @@
+from contextlib import ExitStack
+
+import concourse.mybir as mybir
+from concourse.masks import make_identity
+
+K, L, S, T, N = 1024, 512, 512, 512, 512
+FLOPS = 2 * (K + L) * N * S
+
+F32 = mybir.dt.float32
+BF16 = mybir.dt.bfloat16
+I32 = mybir.dt.int32
+U32 = mybir.dt.uint32
+U16 = mybir.dt.uint16
+U8 = mybir.dt.uint8
+FP8X4 = mybir.dt.float8_e4m3fn_x4
+FP4X4 = mybir.dt.float4_e2m1fn_x4
+MULT = mybir.AluOpType.mult
+ADD = mybir.AluOpType.add
+
+P = 128
+PACK = 4
+BLOCKS = N // P
+PASSES = K // (P * PACK)
+HALF = T // 2
+M_VECTOR = 64
+
+
+def tile_moe_heads_combine_two_buffers_kernel(
+    tc, xa_words, xa_scales, wa, xb_words, xb_scales, wb_words, wb_scales, ga, gb, offs, offs2, out
+):
+    nc = tc.nc
+    with ExitStack() as ctx:
+        keep = ctx.enter_context(tc.tile_pool(name="keep", bufs=1))
+        psum = ctx.enter_context(tc.psum_pool(name="psum", bufs=1))
+
+        list_a = keep.tile([P, T // 16], U16, name="list_a")
+        list_b = keep.tile([P, T // 16], U16, name="list_b")
+        wb_plane_raw = keep.tile([P, N], U8, name="wb_plane_raw", align_bytes=64)
+        wb_plane = keep.tile([P, N], U8, name="wb_plane", align_bytes=64)
+        xb_plane = keep.tile([P, S], U8, name="xb_plane", align_bytes=64)
+        xa_plane = keep.tile([P, PASSES * S], U8, name="xa_plane", align_bytes=64)
+        wb_raw = keep.tile([P, N], I32, name="wb_raw", align_bytes=64)
+        wb_codes = keep.tile([P, N], I32, name="wb_codes", align_bytes=64)
+        xb_codes = keep.tile([P, 2 * S], U8, name="xb_codes", align_bytes=64)
+        xa_codes = keep.tile([P, PASSES * S], I32, name="xa_codes", align_bytes=64)
+        wa_raw = [keep.tile([P, PACK * N], F32, name=f"wa_raw{z}", align_bytes=64) for z in range(PASSES)]
+        wa_bf = [keep.tile([P, PACK * N], BF16, name=f"wa_bf{z}", tag=f"wa_bf{z}", align_bytes=64) for z in range(PASSES)]
+        wa_codes = [keep.tile([P, N], U32, name=f"wa_codes{z}", align_bytes=64) for z in range(PASSES)]
+        wa_plane = [keep.tile([P, N], U8, name=f"wa_plane{z}", align_bytes=64) for z in range(PASSES)]
+        ident = keep.tile([P, P], F32, name="ident")
+        ga_col = keep.tile([P, PACK], F32, name="ga_col")
+        gb_col = keep.tile([P, PACK], F32, name="gb_col")
+        ga_all = keep.tile([P, T], F32, name="ga_all")
+        gb_all = keep.tile([P, T], F32, name="gb_all")
+        za = [keep.tile([P, S], F32, name=f"za{j}") for j in range(BLOCKS)]
+        zb = [keep.tile([P, S], F32, name=f"zb{j}") for j in range(BLOCKS)]
+        ya = [keep.tile([P, T], F32, name=f"ya{j}") for j in range(BLOCKS)]
+        yb = [[keep.tile([P, HALF], F32, name=f"yb{j}_{h}") for h in range(2)] for j in range(BLOCKS - 1)]
+        res = [keep.tile([P, T], F32, name=f"res{j}") for j in range(BLOCKS)]
+
+        nc.vector.memset(wb_plane_raw[:].bitcast(I32), 0)
+        nc.vector.memset(xb_plane[:].bitcast(I32), 0)
+        nc.vector.memset(ident[:], 0.0)
+        nc.vector.memset(xa_plane[:].bitcast(I32), 0)
+
+        def load_plane(engine, plane, scales):
+            passes = scales.shape[0]
+            rows = scales.bitcast(I32).rearrange("z (q r) c -> r q z c", r=4)
+            view = plane[:].bitcast(I32).rearrange("p (z c) -> p z c", z=passes)
+            for r in range(4):
+                engine.dma_start(out=view[r:P:32], in_=rows[r])
+
+        make_identity(nc, ident[:], nomemset=True)
+
+        nc.sync.dma_start(out=wb_raw[:], in_=wb_words[0].rearrange("p n t -> p (n t)").bitcast(I32))
+        nc.sync.dma_start(out=gb_col[:], in_=gb.rearrange("o (p c) -> (o p) c", c=PACK))
+        nc.sync.dma_start(out=ga_col[:], in_=ga.rearrange("o (p c) -> (o p) c", c=PACK))
+        nc.sync.dma_start(out=xb_codes[:].bitcast(I32), in_=xb_words[0].bitcast(I32))
+        load_plane(nc.sync, wb_plane_raw, wb_scales)
+        load_plane(nc.sync, xb_plane, xb_scales)
+        nc.sync.dma_start(list_b[:], offs2)
+        wa_rows = wa.rearrange("(z p r) n -> z p (r n)", z=PASSES, r=PACK)
+        for z in range(PASSES):
+            nc.sync.dma_start(out=wa_raw[z][:], in_=wa_rows[z])
+        nc.sync.dma_start(
+            out=xa_codes[:].rearrange("p (z n) -> p z n", z=PASSES),
+            in_=xa_words.rearrange("z p n t -> p z (n t)").bitcast(I32),
+        )
+        load_plane(nc.sync, xa_plane, xa_scales)
+        nc.sync.dma_start(list_a[:], offs)
+
+        def by_block(ap):
+            return ap.rearrange("p (j m) -> p m j", j=BLOCKS)
+
+        def as_stored(ap):
+            return ap.rearrange("p (m j) -> p m j", j=BLOCKS)
+
+        nc.vector.tensor_copy(out=by_block(wb_plane[:]), in_=as_stored(wb_plane_raw[:]))
+        nc.vector.tensor_copy(out=by_block(wb_codes[:]), in_=as_stored(wb_raw[:]))
+
+        def spread_gate(col, full, tag):
+            bank = psum.tile([P, T], F32, name=tag, tag=tag)
+            for c in range(PACK):
+                nc.tensor.transpose(bank[:, c * P : (c + 1) * P], col[:, c : c + 1].to_broadcast([P, P]), ident[:])
+            nc.vector.tensor_copy(
+                out=full[:].rearrange("q (p c) -> q p c", c=PACK), in_=bank[:].rearrange("q (c p) -> q p c", c=PACK)
+            )
+
+        spread_gate(gb_col, gb_all, "bank_a0")
+        spread_gate(ga_col, ga_all, "bank_a1")
+
+        for j in range(BLOCKS):
+            cols = slice(j * P, (j + 1) * P)
+            bank = psum.tile([P, S], F32, name=f"bank_b{j}", tag=f"bank_b{j}")
+            nc.tensor.matmul_mx(
+                out=bank[:],
+                lhsT=wb_codes[:, cols].bitcast(FP8X4),
+                lhsT_scale=wb_plane[:, cols],
+                rhs=xb_codes[:].bitcast(FP4X4),
+                rhs_scale=xb_plane[:],
+                start=True,
+                stop=True,
+            )
+            nc.scalar.copy(out=zb[j][:], in_=bank[:])
+
+        def cast(copy, z, m0, m1):
+            copy(
+                out=wa_bf[z][:].rearrange("p (j m r) -> p m r j", j=BLOCKS, r=PACK)[:, m0:m1],
+                in_=wa_raw[z][:].rearrange("p (r m j) -> p m r j", j=BLOCKS, r=PACK)[:, m0:m1],
+            )
+
+        def quantize(z, j0, j1):
+            nc.vector.quantize_mx(
+                out=wa_codes[z][:, j0 * P : j1 * P].bitcast(FP8X4),
+                scales=wa_plane[z][:, j0 * P : j1 * P],
+                in_=wa_bf[z][:, j0 * P * PACK : j1 * P * PACK],
+            )
+
+        def gather(dst, window, offsets, gate, h):
+            nc.vector.tensor_tensor(
+                dst,
+                window[:].indirect(offsets[:, h * HALF // 16 : (h + 1) * HALF // 16]),
+                gate[:, h * HALF : (h + 1) * HALF],
+                MULT,
+            )
+
+        cast(nc.scalar.copy, 0, 0, P // 2)
+        cast(nc.scalar.copy, 0, P // 2, P)
+        for j in range(BLOCKS - 1):
+            for h in range(2):
+                gather(yb[j][h][:], zb[j], list_b, gb_all, h)
+        cast(nc.vector.tensor_copy, 1, 0, M_VECTOR)
+        cast(nc.scalar.copy, 1, M_VECTOR, P)
+        quantize(0, 0, BLOCKS)
+        yb_last0 = keep.tile([P, HALF], F32, name="yb_last0", tag="wa_bf0", align_bytes=64)
+        gather(yb_last0[:], zb[BLOCKS - 1], list_b, gb_all, 0)
+        quantize(1, 0, 2)
+        quantize(1, 2, BLOCKS)
+        yb_last1 = keep.tile([P, HALF], F32, name="yb_last1", tag="wa_bf1", align_bytes=64)
+        gather(yb_last1[:], zb[BLOCKS - 1], list_b, gb_all, 1)
+        yb.append([yb_last0, yb_last1])
+
+        for j in range(BLOCKS):
+            cols = slice(j * P, (j + 1) * P)
+            bank = psum.tile([P, S], F32, name=f"bank_a{j}", tag=f"bank_a{j}")
+            for z in range(PASSES):
+                nc.tensor.matmul_mx(
+                    out=bank[:],
+                    lhsT=wa_codes[z][:, cols].bitcast(FP8X4),
+                    lhsT_scale=wa_plane[z][:, cols],
+                    rhs=xa_codes[:, z * S : (z + 1) * S].bitcast(FP8X4),
+                    rhs_scale=xa_plane[:, z * S : (z + 1) * S],
+                    start=(z == 0),
+                    stop=(z == PASSES - 1),
+                )
+            nc.scalar.copy(out=za[j][:], in_=bank[:])
+
+        out_rows = out.rearrange("(p j) t -> j p t", j=BLOCKS)
+
+        for j in range(BLOCKS):
+            for h in range(2):
+                gather(ya[j][:, h * HALF : (h + 1) * HALF], za[j], list_a, ga_all, h)
+            for h in range(2):
+                cols = slice(h * HALF, (h + 1) * HALF)
+                nc.vector.tensor_tensor(res[j][:, cols], ya[j][:, cols], yb[j][h][:], ADD)
+                if j == BLOCKS - 1:
+                    nc.sync.dma_start(out=out_rows[j][:, cols], in_=res[j][:, cols])
+            if j < BLOCKS - 1:
+                nc.sync.dma_start(out=out_rows[j], in_=res[j][:])

@@ -22,7 +22,8 @@ PACK = 4
 BLOCKS = N // P
 PASSES = K // (P * PACK)
 HALF = T // 2
-M_VECTOR = 64
+PE_UNITS = 4
+M_VECTOR = 32
 
 
 def tile_moe_heads_combine_two_buffers_kernel(
@@ -35,6 +36,7 @@ def tile_moe_heads_combine_two_buffers_kernel(
 
         list_a = keep.tile([P, T // 16], U16, name="list_a")
         list_b = keep.tile([P, T // 16], U16, name="list_b")
+        wb_rows = keep.tile([P, N // 4], I32, name="wb_rows", align_bytes=64)
         wb_plane_raw = keep.tile([P, N], U8, name="wb_plane_raw", align_bytes=64)
         wb_plane = keep.tile([P, N], U8, name="wb_plane", align_bytes=64)
         xb_plane = keep.tile([P, S], U8, name="xb_plane", align_bytes=64)
@@ -43,7 +45,8 @@ def tile_moe_heads_combine_two_buffers_kernel(
         wb_codes = keep.tile([P, N], I32, name="wb_codes", align_bytes=64)
         xb_codes = keep.tile([P, 2 * S], U8, name="xb_codes", align_bytes=64)
         xa_codes = keep.tile([P, PASSES * S], I32, name="xa_codes", align_bytes=64)
-        wa_raw = [keep.tile([P, PACK * N], F32, name=f"wa_raw{z}", align_bytes=64) for z in range(PASSES)]
+        wa_first = [keep.tile([P, PACK * N // 2], F32, name=f"wa_first{i}", align_bytes=64) for i in range(2)]
+        wa_last = keep.tile([P, PACK * N], F32, name="wa_last", align_bytes=64)
         wa_bf = [keep.tile([P, PACK * N], BF16, name=f"wa_bf{z}", tag=f"wa_bf{z}", align_bytes=64) for z in range(PASSES)]
         wa_codes = [keep.tile([P, N], U32, name=f"wa_codes{z}", align_bytes=64) for z in range(PASSES)]
         wa_plane = [keep.tile([P, N], U8, name=f"wa_plane{z}", align_bytes=64) for z in range(PASSES)]
@@ -55,38 +58,44 @@ def tile_moe_heads_combine_two_buffers_kernel(
         za = [keep.tile([P, S], F32, name=f"za{j}") for j in range(BLOCKS)]
         zb = [keep.tile([P, S], F32, name=f"zb{j}") for j in range(BLOCKS)]
         ya = [keep.tile([P, T], F32, name=f"ya{j}") for j in range(BLOCKS)]
-        yb = [[keep.tile([P, HALF], F32, name=f"yb{j}_{h}") for h in range(2)] for j in range(BLOCKS - 1)]
+        yb = [keep.tile([P, T], F32, name=f"yb{j}") for j in range(BLOCKS - 1)]
+        turned = [keep.tile([P, HALF], F32, name=f"turned{u}") for u in range(PE_UNITS)]
         res = [keep.tile([P, T], F32, name=f"res{j}") for j in range(BLOCKS)]
 
-        nc.vector.memset(wb_plane_raw[:].bitcast(I32), 0)
         nc.vector.memset(xb_plane[:].bitcast(I32), 0)
+        nc.vector.memset(wb_plane_raw[:].bitcast(I32), 0)
         nc.vector.memset(ident[:], 0.0)
         nc.vector.memset(xa_plane[:].bitcast(I32), 0)
 
         def load_plane(engine, plane, scales):
             passes = scales.shape[0]
             rows = scales.bitcast(I32).rearrange("z (q r) c -> r q z c", r=4)
-            view = plane[:].bitcast(I32).rearrange("p (z c) -> p z c", z=passes)
+            view = plane.rearrange("p (z c) -> p z c", z=passes)
             for r in range(4):
                 engine.dma_start(out=view[r:P:32], in_=rows[r])
 
         make_identity(nc, ident[:], nomemset=True)
 
+        load_plane(nc.sync, wb_rows[:], wb_scales)
         nc.sync.dma_start(out=wb_raw[:], in_=wb_words[0].rearrange("p n t -> p (n t)").bitcast(I32))
         nc.sync.dma_start(out=gb_col[:], in_=gb.rearrange("o (p c) -> (o p) c", c=PACK))
-        nc.sync.dma_start(out=ga_col[:], in_=ga.rearrange("o (p c) -> (o p) c", c=PACK))
         nc.sync.dma_start(out=xb_codes[:].bitcast(I32), in_=xb_words[0].bitcast(I32))
-        load_plane(nc.sync, wb_plane_raw, wb_scales)
-        load_plane(nc.sync, xb_plane, xb_scales)
+        wa_rows = wa.rearrange("(z p r) n -> z p r n", z=PASSES, r=PACK)
+
+        def by_row(tile):
+            return tile[:].rearrange("p (r n) -> p r n", r=PACK)
+
+        nc.sync.dma_start(out=by_row(wa_first[0]), in_=wa_rows[0][:, :, 0 : N // 2])
+        load_plane(nc.sync, xb_plane[:].bitcast(I32), xb_scales)
         nc.sync.dma_start(list_b[:], offs2)
-        wa_rows = wa.rearrange("(z p r) n -> z p (r n)", z=PASSES, r=PACK)
-        for z in range(PASSES):
-            nc.sync.dma_start(out=wa_raw[z][:], in_=wa_rows[z])
+        nc.sync.dma_start(out=by_row(wa_first[1]), in_=wa_rows[0][:, :, N // 2 : N])
+        nc.sync.dma_start(out=by_row(wa_last), in_=wa_rows[1])
+        nc.sync.dma_start(out=ga_col[:], in_=ga.rearrange("o (p c) -> (o p) c", c=PACK))
         nc.sync.dma_start(
             out=xa_codes[:].rearrange("p (z n) -> p z n", z=PASSES),
             in_=xa_words.rearrange("z p n t -> p z (n t)").bitcast(I32),
         )
-        load_plane(nc.sync, xa_plane, xa_scales)
+        load_plane(nc.sync, xa_plane[:].bitcast(I32), xa_scales)
         nc.sync.dma_start(list_a[:], offs)
 
         def by_block(ap):
@@ -95,38 +104,45 @@ def tile_moe_heads_combine_two_buffers_kernel(
         def as_stored(ap):
             return ap.rearrange("p (m j) -> p m j", j=BLOCKS)
 
+        for q in range(4):
+            live = slice(32 * q, 32 * q + 4)
+            nc.vector.tensor_copy(out=wb_plane_raw[live, :].bitcast(I32), in_=wb_rows[live, :])
         nc.vector.tensor_copy(out=by_block(wb_plane[:]), in_=as_stored(wb_plane_raw[:]))
         nc.vector.tensor_copy(out=by_block(wb_codes[:]), in_=as_stored(wb_raw[:]))
 
-        def spread_gate(col, full, tag):
+        def spread_gate(copy, col, full, tag):
             bank = psum.tile([P, T], F32, name=tag, tag=tag)
             for c in range(PACK):
                 nc.tensor.transpose(bank[:, c * P : (c + 1) * P], col[:, c : c + 1].to_broadcast([P, P]), ident[:])
-            nc.vector.tensor_copy(
+            copy(
                 out=full[:].rearrange("q (p c) -> q p c", c=PACK), in_=bank[:].rearrange("q (c p) -> q p c", c=PACK)
             )
 
-        spread_gate(gb_col, gb_all, "bank_a0")
-        spread_gate(ga_col, ga_all, "bank_a1")
+        spread_gate(nc.vector.tensor_copy, gb_col, gb_all, "bank_a0")
 
-        for j in range(BLOCKS):
+        def product_b(copy, j, s0, s1, tag):
             cols = slice(j * P, (j + 1) * P)
-            bank = psum.tile([P, S], F32, name=f"bank_b{j}", tag=f"bank_b{j}")
+            bank = psum.tile([P, s1 - s0], F32, name=f"zb_sum{j}_{s0}", tag=tag)
             nc.tensor.matmul_mx(
                 out=bank[:],
                 lhsT=wb_codes[:, cols].bitcast(FP8X4),
                 lhsT_scale=wb_plane[:, cols],
-                rhs=xb_codes[:].bitcast(FP4X4),
-                rhs_scale=xb_plane[:],
+                rhs=xb_codes[:, 2 * s0 : 2 * s1].bitcast(FP4X4),
+                rhs_scale=xb_plane[:, s0:s1],
                 start=True,
                 stop=True,
             )
-            nc.scalar.copy(out=zb[j][:], in_=bank[:])
+            copy(out=zb[j][:, s0:s1], in_=bank[:])
 
-        def cast(copy, z, m0, m1):
+        product_b(nc.vector.tensor_copy, 0, 0, S // 2, "bank_b0")
+        product_b(nc.vector.tensor_copy, 0, S // 2, S, "bank_a2")
+        for j in range(1, BLOCKS):
+            product_b(nc.scalar.copy, j, 0, S, f"bank_b{j}")
+
+        def cast(copy, z, m0, m1, raw, m_raw):
             copy(
                 out=wa_bf[z][:].rearrange("p (j m r) -> p m r j", j=BLOCKS, r=PACK)[:, m0:m1],
-                in_=wa_raw[z][:].rearrange("p (r m j) -> p m r j", j=BLOCKS, r=PACK)[:, m0:m1],
+                in_=raw[:].rearrange("p (r m j) -> p m r j", j=BLOCKS, r=PACK)[:, m0 - m_raw : m1 - m_raw],
             )
 
         def quantize(z, j0, j1):
@@ -144,21 +160,40 @@ def tile_moe_heads_combine_two_buffers_kernel(
                 MULT,
             )
 
-        cast(nc.scalar.copy, 0, 0, P // 2)
-        cast(nc.scalar.copy, 0, P // 2, P)
+        for i in range(2):
+            cast(nc.scalar.copy, 0, i * P // 2, (i + 1) * P // 2, wa_first[i], i * P // 2)
         for j in range(BLOCKS - 1):
             for h in range(2):
-                gather(yb[j][h][:], zb[j], list_b, gb_all, h)
-        cast(nc.vector.tensor_copy, 1, 0, M_VECTOR)
-        cast(nc.scalar.copy, 1, M_VECTOR, P)
+                gather(yb[j][:, h * HALF : (h + 1) * HALF], zb[j], list_b, gb_all, h)
+        cast(nc.vector.tensor_copy, 1, 0, M_VECTOR, wa_last, 0)
+        cast(nc.scalar.copy, 1, M_VECTOR, P, wa_last, 0)
+        spread_gate(nc.scalar.copy, ga_col, ga_all, "bank_a1")
         quantize(0, 0, BLOCKS)
-        yb_last0 = keep.tile([P, HALF], F32, name="yb_last0", tag="wa_bf0", align_bytes=64)
-        gather(yb_last0[:], zb[BLOCKS - 1], list_b, gb_all, 0)
-        quantize(1, 0, 2)
-        quantize(1, 2, BLOCKS)
-        yb_last1 = keep.tile([P, HALF], F32, name="yb_last1", tag="wa_bf1", align_bytes=64)
-        gather(yb_last1[:], zb[BLOCKS - 1], list_b, gb_all, 1)
-        yb.append([yb_last0, yb_last1])
+        quantize(1, 0, BLOCKS)
+        yb_last = keep.tile([P, T], F32, name="yb_last", tag="wa_bf1", align_bytes=64)
+        for h in range(2):
+            gather(yb_last[:, h * HALF : (h + 1) * HALF], zb[BLOCKS - 1], list_b, gb_all, h)
+        yb.append(yb_last)
+
+        def turn(bank, src, opens, closes):
+            for c in range(HALF // P):
+                cols = slice(c * P, (c + 1) * P)
+                nc.tensor.matmul(
+                    bank[:, cols],
+                    lhsT=src[:, cols],
+                    rhs=ident[:],
+                    start=opens and c == 0,
+                    stop=closes and c == HALF // P - 1,
+                    is_transpose=True,
+                )
+
+        def open_sum(u):
+            j, h = divmod(u, 2)
+            bank = psum.tile([P, HALF], F32, name=f"sum{u}", tag=f"bank_b{u % BLOCKS}")
+            turn(bank, yb[j][:, h * HALF : (h + 1) * HALF], True, False)
+            return bank
+
+        sums = [open_sum(u) for u in range(BLOCKS)]
 
         for j in range(BLOCKS):
             cols = slice(j * P, (j + 1) * P)
@@ -181,9 +216,17 @@ def tile_moe_heads_combine_two_buffers_kernel(
             for h in range(2):
                 gather(ya[j][:, h * HALF : (h + 1) * HALF], za[j], list_a, ga_all, h)
             for h in range(2):
+                u = 2 * j + h
                 cols = slice(h * HALF, (h + 1) * HALF)
-                nc.vector.tensor_tensor(res[j][:, cols], ya[j][:, cols], yb[j][h][:], ADD)
-                if j == BLOCKS - 1:
+                if u < PE_UNITS:
+                    turn(sums[u], ya[j][:, cols], False, True)
+                    nc.scalar.copy(out=turned[u][:], in_=sums[u][:])
+                    if u + BLOCKS < PE_UNITS:
+                        sums.append(open_sum(u + BLOCKS))
+                    back = psum.tile([P, HALF], F32, name=f"back{u}", tag=f"bank_a{u % BLOCKS}")
+                    turn(back, turned[u][:], True, True)
+                    nc.scalar.copy(out=res[j][:, cols], in_=back[:])
+                    nc.scalar.dma_start(out=out_rows[j][:, cols], in_=res[j][:, cols])
+                else:
+                    nc.vector.tensor_tensor(res[j][:, cols], ya[j][:, cols], yb[j][:, cols], ADD)
                     nc.sync.dma_start(out=out_rows[j][:, cols], in_=res[j][:, cols])
-            if j < BLOCKS - 1:
-                nc.sync.dma_start(out=out_rows[j], in_=res[j][:])

@@ -23,7 +23,7 @@ BLOCKS = N // P
 PASSES = K // (P * PACK)
 HALF = T // 2
 PE_UNITS = 4
-M_VECTOR = 32
+M_VECTOR = 56
 
 
 def tile_moe_heads_combine_two_buffers_kernel(
@@ -56,7 +56,7 @@ def tile_moe_heads_combine_two_buffers_kernel(
         ga_all = keep.tile([P, T], F32, name="ga_all")
         gb_all = keep.tile([P, T], F32, name="gb_all")
         za = [keep.tile([P, S], F32, name=f"za{j}") for j in range(BLOCKS)]
-        zb = [keep.tile([P, S], F32, name=f"zb{j}") for j in range(BLOCKS)]
+        zb = [keep.tile([P, 2 * S], F32, name=f"zb{j}") for j in range(BLOCKS)]
         ya = [keep.tile([P, T], F32, name=f"ya{j}") for j in range(BLOCKS)]
         yb = [keep.tile([P, T], F32, name=f"yb{j}") for j in range(BLOCKS - 1)]
         turned = [keep.tile([P, HALF], F32, name=f"turned{u}") for u in range(PE_UNITS)]
@@ -163,16 +163,15 @@ def tile_moe_heads_combine_two_buffers_kernel(
         for i in range(2):
             cast(nc.scalar.copy, 0, i * P // 2, (i + 1) * P // 2, wa_first[i], i * P // 2)
         for j in range(BLOCKS - 1):
-            for h in range(2):
-                gather(yb[j][:, h * HALF : (h + 1) * HALF], zb[j], list_b, gb_all, h)
+            nc.vector.tensor_tensor(yb[j][:], zb[j][:].indirect(list_b[:]), gb_all[:], MULT)
         cast(nc.vector.tensor_copy, 1, 0, M_VECTOR, wa_last, 0)
         cast(nc.scalar.copy, 1, M_VECTOR, P, wa_last, 0)
         spread_gate(nc.scalar.copy, ga_col, ga_all, "bank_a1")
         quantize(0, 0, BLOCKS)
-        quantize(1, 0, BLOCKS)
+        quantize(1, 0, BLOCKS // 2)
+        quantize(1, BLOCKS // 2, BLOCKS)
         yb_last = keep.tile([P, T], F32, name="yb_last", tag="wa_bf1", align_bytes=64)
-        for h in range(2):
-            gather(yb_last[:, h * HALF : (h + 1) * HALF], zb[BLOCKS - 1], list_b, gb_all, h)
+        nc.vector.tensor_tensor(yb_last[:], zb[BLOCKS - 1][:].indirect(list_b[:]), gb_all[:], MULT)
         yb.append(yb_last)
 
         def turn(bank, src, opens, closes):

@@ -47,9 +47,9 @@ def tile_moe_heads_combine_two_buffers_kernel(
         xa_codes = keep.tile([P, PASSES * S], I32, name="xa_codes", align_bytes=64)
         wa_first = [keep.tile([P, PACK * N // 2], F32, name=f"wa_first{i}", align_bytes=64) for i in range(2)]
         wa_last = keep.tile([P, PACK * N], F32, name="wa_last", align_bytes=64)
-        wa_bf = [keep.tile([P, PACK * N], BF16, name=f"wa_bf{z}", tag=f"wa_bf{z}", align_bytes=64) for z in range(PASSES)]
-        wa_codes = [keep.tile([P, N], U32, name=f"wa_codes{z}", align_bytes=64) for z in range(PASSES)]
-        wa_plane = [keep.tile([P, N], U8, name=f"wa_plane{z}", align_bytes=64) for z in range(PASSES)]
+        wa_bf = keep.tile([P, PASSES * PACK * N], BF16, name="wa_bf", tag="wa_bf", align_bytes=64)
+        wa_codes = keep.tile([P, PASSES * N], U32, name="wa_codes", align_bytes=64)
+        wa_plane = keep.tile([P, PASSES * N], U8, name="wa_plane", align_bytes=64)
         ident = keep.tile([P, P], F32, name="ident")
         ga_col = keep.tile([P, PACK], F32, name="ga_col")
         gb_col = keep.tile([P, PACK], F32, name="gb_col")
@@ -141,15 +141,16 @@ def tile_moe_heads_combine_two_buffers_kernel(
 
         def cast(copy, z, m0, m1, raw, m_raw):
             copy(
-                out=wa_bf[z][:].rearrange("p (j m r) -> p m r j", j=BLOCKS, r=PACK)[:, m0:m1],
+                out=wa_bf[:].rearrange("p (j z m r) -> p z m r j", j=BLOCKS, z=PASSES, r=PACK)[:, z, m0:m1],
                 in_=raw[:].rearrange("p (r m j) -> p m r j", j=BLOCKS, r=PACK)[:, m0 - m_raw : m1 - m_raw],
             )
 
-        def quantize(z, j0, j1):
+        def quantize(j):
+            words = slice(j * PASSES * P, (j + 1) * PASSES * P)
             nc.vector.quantize_mx(
-                out=wa_codes[z][:, j0 * P : j1 * P].bitcast(FP8X4),
-                scales=wa_plane[z][:, j0 * P : j1 * P],
-                in_=wa_bf[z][:, j0 * P * PACK : j1 * P * PACK],
+                out=wa_codes[:, words].bitcast(FP8X4),
+                scales=wa_plane[:, words],
+                in_=wa_bf[:, words.start * PACK : words.stop * PACK],
             )
 
         def gather(dst, window, offsets, gate, h):
@@ -167,10 +168,9 @@ def tile_moe_heads_combine_two_buffers_kernel(
         cast(nc.vector.tensor_copy, 1, 0, M_VECTOR, wa_last, 0)
         cast(nc.scalar.copy, 1, M_VECTOR, P, wa_last, 0)
         spread_gate(nc.scalar.copy, ga_col, ga_all, "bank_a1")
-        quantize(0, 0, BLOCKS)
-        quantize(1, 0, BLOCKS // 2)
-        quantize(1, BLOCKS // 2, BLOCKS)
-        yb_last = keep.tile([P, T], F32, name="yb_last", tag="wa_bf1", align_bytes=64)
+        for j in range(BLOCKS):
+            quantize(j)
+        yb_last = keep.tile([P, T], F32, name="yb_last", tag="wa_bf", align_bytes=64)
         nc.vector.tensor_tensor(yb_last[:], zb[BLOCKS - 1][:].indirect(list_b[:]), gb_all[:], MULT)
         yb.append(yb_last)
 
@@ -195,13 +195,13 @@ def tile_moe_heads_combine_two_buffers_kernel(
         sums = [open_sum(u) for u in range(BLOCKS)]
 
         for j in range(BLOCKS):
-            cols = slice(j * P, (j + 1) * P)
             bank = psum.tile([P, S], F32, name=f"bank_a{j}", tag=f"bank_a{j}")
             for z in range(PASSES):
+                cols = slice((j * PASSES + z) * P, (j * PASSES + z + 1) * P)
                 nc.tensor.matmul_mx(
                     out=bank[:],
-                    lhsT=wa_codes[z][:, cols].bitcast(FP8X4),
-                    lhsT_scale=wa_plane[z][:, cols],
+                    lhsT=wa_codes[:, cols].bitcast(FP8X4),
+                    lhsT_scale=wa_plane[:, cols],
                     rhs=xa_codes[:, z * S : (z + 1) * S].bitcast(FP8X4),
                     rhs_scale=xa_plane[:, z * S : (z + 1) * S],
                     start=(z == 0),

from contextlib import ExitStack

import concourse.mybir as mybir
from concourse.masks import make_identity

K, L, S, T, N = 1024, 512, 512, 512, 512
FLOPS = 2 * (K + L) * N * S

F32 = mybir.dt.float32
BF16 = mybir.dt.bfloat16
I32 = mybir.dt.int32
U32 = mybir.dt.uint32
U16 = mybir.dt.uint16
U8 = mybir.dt.uint8
FP8X4 = mybir.dt.float8_e4m3fn_x4
FP4X4 = mybir.dt.float4_e2m1fn_x4
MULT = mybir.AluOpType.mult
ADD = mybir.AluOpType.add

P = 128
PACK = 4
BLOCKS = N // P
PASSES = K // (P * PACK)
HALF = T // 2
PE_UNITS = 4
M_VECTOR = 56


def tile_moe_heads_combine_two_buffers_kernel(
    tc, xa_words, xa_scales, wa, xb_words, xb_scales, wb_words, wb_scales, ga, gb, offs, offs2, out
):
    nc = tc.nc
    with ExitStack() as ctx:
        keep = ctx.enter_context(tc.tile_pool(name="keep", bufs=1))
        psum = ctx.enter_context(tc.psum_pool(name="psum", bufs=1))

        list_a = keep.tile([P, T // 16], U16, name="list_a")
        list_b = keep.tile([P, T // 16], U16, name="list_b")
        wb_rows = keep.tile([P, N // 4], I32, name="wb_rows", align_bytes=64)
        wb_plane_raw = keep.tile([P, N], U8, name="wb_plane_raw", align_bytes=64)
        wb_plane = keep.tile([P, N], U8, name="wb_plane", align_bytes=64)
        xb_plane = keep.tile([P, S], U8, name="xb_plane", align_bytes=64)
        xa_plane = keep.tile([P, PASSES * S], U8, name="xa_plane", align_bytes=64)
        wb_raw = keep.tile([P, N], I32, name="wb_raw", align_bytes=64)
        wb_codes = keep.tile([P, N], I32, name="wb_codes", align_bytes=64)
        xb_codes = keep.tile([P, 2 * S], U8, name="xb_codes", align_bytes=64)
        xa_codes = keep.tile([P, PASSES * S], I32, name="xa_codes", align_bytes=64)
        wa_first = [keep.tile([P, PACK * N // 2], F32, name=f"wa_first{i}", align_bytes=64) for i in range(2)]
        wa_last = keep.tile([P, PACK * N], F32, name="wa_last", align_bytes=64)
        wa_bf = keep.tile([P, PASSES * PACK * N], BF16, name="wa_bf", tag="wa_bf", align_bytes=64)
        wa_codes = keep.tile([P, PASSES * N], U32, name="wa_codes", align_bytes=64)
        wa_plane = keep.tile([P, PASSES * N], U8, name="wa_plane", align_bytes=64)
        ident = keep.tile([P, P], F32, name="ident")
        ga_col = keep.tile([P, PACK], F32, name="ga_col")
        gb_col = keep.tile([P, PACK], F32, name="gb_col")
        ga_all = keep.tile([P, T], F32, name="ga_all")
        gb_all = keep.tile([P, T], F32, name="gb_all")
        za = [keep.tile([P, S], F32, name=f"za{j}") for j in range(BLOCKS)]
        zb = [keep.tile([P, 2 * S], F32, name=f"zb{j}") for j in range(BLOCKS)]
        ya = [keep.tile([P, T], F32, name=f"ya{j}") for j in range(BLOCKS)]
        yb = [keep.tile([P, T], F32, name=f"yb{j}") for j in range(BLOCKS - 1)]
        turned = [keep.tile([P, HALF], F32, name=f"turned{u}") for u in range(PE_UNITS)]
        res = [keep.tile([P, T], F32, name=f"res{j}") for j in range(BLOCKS)]

        nc.vector.memset(xb_plane[:].bitcast(I32), 0)
        nc.vector.memset(wb_plane_raw[:].bitcast(I32), 0)
        nc.vector.memset(ident[:], 0.0)
        nc.vector.memset(xa_plane[:].bitcast(I32), 0)

        def load_plane(engine, plane, scales):
            passes = scales.shape[0]
            rows = scales.bitcast(I32).rearrange("z (q r) c -> r q z c", r=4)
            view = plane.rearrange("p (z c) -> p z c", z=passes)
            for r in range(4):
                engine.dma_start(out=view[r:P:32], in_=rows[r])

        make_identity(nc, ident[:], nomemset=True)

        load_plane(nc.sync, wb_rows[:], wb_scales)
        nc.sync.dma_start(out=wb_raw[:], in_=wb_words[0].rearrange("p n t -> p (n t)").bitcast(I32))
        nc.sync.dma_start(out=gb_col[:], in_=gb.rearrange("o (p c) -> (o p) c", c=PACK))
        nc.sync.dma_start(out=xb_codes[:].bitcast(I32), in_=xb_words[0].bitcast(I32))
        wa_rows = wa.rearrange("(z p r) n -> z p r n", z=PASSES, r=PACK)

        def by_row(tile):
            return tile[:].rearrange("p (r n) -> p r n", r=PACK)

        nc.sync.dma_start(out=by_row(wa_first[0]), in_=wa_rows[0][:, :, 0 : N // 2])
        load_plane(nc.sync, xb_plane[:].bitcast(I32), xb_scales)
        nc.sync.dma_start(list_b[:], offs2)
        nc.sync.dma_start(out=by_row(wa_first[1]), in_=wa_rows[0][:, :, N // 2 : N])
        nc.sync.dma_start(out=by_row(wa_last), in_=wa_rows[1])
        nc.sync.dma_start(out=ga_col[:], in_=ga.rearrange("o (p c) -> (o p) c", c=PACK))
        nc.sync.dma_start(
            out=xa_codes[:].rearrange("p (z n) -> p z n", z=PASSES),
            in_=xa_words.rearrange("z p n t -> p z (n t)").bitcast(I32),
        )
        load_plane(nc.sync, xa_plane[:].bitcast(I32), xa_scales)
        nc.sync.dma_start(list_a[:], offs)

        def by_block(ap):
            return ap.rearrange("p (j m) -> p m j", j=BLOCKS)

        def as_stored(ap):
            return ap.rearrange("p (m j) -> p m j", j=BLOCKS)

        for q in range(4):
            live = slice(32 * q, 32 * q + 4)
            nc.vector.tensor_copy(out=wb_plane_raw[live, :].bitcast(I32), in_=wb_rows[live, :])
        nc.vector.tensor_copy(out=by_block(wb_plane[:]), in_=as_stored(wb_plane_raw[:]))
        nc.vector.tensor_copy(out=by_block(wb_codes[:]), in_=as_stored(wb_raw[:]))

        def spread_gate(copy, col, full, tag):
            bank = psum.tile([P, T], F32, name=tag, tag=tag)
            for c in range(PACK):
                nc.tensor.transpose(bank[:, c * P : (c + 1) * P], col[:, c : c + 1].to_broadcast([P, P]), ident[:])
            copy(
                out=full[:].rearrange("q (p c) -> q p c", c=PACK), in_=bank[:].rearrange("q (c p) -> q p c", c=PACK)
            )

        spread_gate(nc.vector.tensor_copy, gb_col, gb_all, "bank_a0")

        def product_b(copy, j, s0, s1, tag):
            cols = slice(j * P, (j + 1) * P)
            bank = psum.tile([P, s1 - s0], F32, name=f"zb_sum{j}_{s0}", tag=tag)
            nc.tensor.matmul_mx(
                out=bank[:],
                lhsT=wb_codes[:, cols].bitcast(FP8X4),
                lhsT_scale=wb_plane[:, cols],
                rhs=xb_codes[:, 2 * s0 : 2 * s1].bitcast(FP4X4),
                rhs_scale=xb_plane[:, s0:s1],
                start=True,
                stop=True,
            )
            copy(out=zb[j][:, s0:s1], in_=bank[:])

        product_b(nc.vector.tensor_copy, 0, 0, S // 2, "bank_b0")
        product_b(nc.vector.tensor_copy, 0, S // 2, S, "bank_a2")
        for j in range(1, BLOCKS):
            product_b(nc.scalar.copy, j, 0, S, f"bank_b{j}")

        def cast(copy, z, m0, m1, raw, m_raw):
            copy(
                out=wa_bf[:].rearrange("p (j z m r) -> p z m r j", j=BLOCKS, z=PASSES, r=PACK)[:, z, m0:m1],
                in_=raw[:].rearrange("p (r m j) -> p m r j", j=BLOCKS, r=PACK)[:, m0 - m_raw : m1 - m_raw],
            )

        def quantize(j):
            words = slice(j * PASSES * P, (j + 1) * PASSES * P)
            nc.vector.quantize_mx(
                out=wa_codes[:, words].bitcast(FP8X4),
                scales=wa_plane[:, words],
                in_=wa_bf[:, words.start * PACK : words.stop * PACK],
            )

        def gather(dst, window, offsets, gate, h):
            nc.vector.tensor_tensor(
                dst,
                window[:].indirect(offsets[:, h * HALF // 16 : (h + 1) * HALF // 16]),
                gate[:, h * HALF : (h + 1) * HALF],
                MULT,
            )

        for i in range(2):
            cast(nc.scalar.copy, 0, i * P // 2, (i + 1) * P // 2, wa_first[i], i * P // 2)
        for j in range(BLOCKS - 1):
            nc.vector.tensor_tensor(yb[j][:], zb[j][:].indirect(list_b[:]), gb_all[:], MULT)
        cast(nc.vector.tensor_copy, 1, 0, M_VECTOR, wa_last, 0)
        cast(nc.scalar.copy, 1, M_VECTOR, P, wa_last, 0)
        spread_gate(nc.scalar.copy, ga_col, ga_all, "bank_a1")
        for j in range(BLOCKS):
            quantize(j)
        yb_last = keep.tile([P, T], F32, name="yb_last", tag="wa_bf", align_bytes=64)
        nc.vector.tensor_tensor(yb_last[:], zb[BLOCKS - 1][:].indirect(list_b[:]), gb_all[:], MULT)
        yb.append(yb_last)

        def turn(bank, src, opens, closes):
            for c in range(HALF // P):
                cols = slice(c * P, (c + 1) * P)
                nc.tensor.matmul(
                    bank[:, cols],
                    lhsT=src[:, cols],
                    rhs=ident[:],
                    start=opens and c == 0,
                    stop=closes and c == HALF // P - 1,
                    is_transpose=True,
                )

        def open_sum(u):
            j, h = divmod(u, 2)
            bank = psum.tile([P, HALF], F32, name=f"sum{u}", tag=f"bank_b{u % BLOCKS}")
            turn(bank, yb[j][:, h * HALF : (h + 1) * HALF], True, False)
            return bank

        sums = [open_sum(u) for u in range(BLOCKS)]

        for j in range(BLOCKS):
            bank = psum.tile([P, S], F32, name=f"bank_a{j}", tag=f"bank_a{j}")
            for z in range(PASSES):
                cols = slice((j * PASSES + z) * P, (j * PASSES + z + 1) * P)
                nc.tensor.matmul_mx(
                    out=bank[:],
                    lhsT=wa_codes[:, cols].bitcast(FP8X4),
                    lhsT_scale=wa_plane[:, cols],
                    rhs=xa_codes[:, z * S : (z + 1) * S].bitcast(FP8X4),
                    rhs_scale=xa_plane[:, z * S : (z + 1) * S],
                    start=(z == 0),
                    stop=(z == PASSES - 1),
                )
            nc.scalar.copy(out=za[j][:], in_=bank[:])

        out_rows = out.rearrange("(p j) t -> j p t", j=BLOCKS)

        for j in range(BLOCKS):
            for h in range(2):
                gather(ya[j][:, h * HALF : (h + 1) * HALF], za[j], list_a, ga_all, h)
            for h in range(2):
                u = 2 * j + h
                cols = slice(h * HALF, (h + 1) * HALF)
                if u < PE_UNITS:
                    turn(sums[u], ya[j][:, cols], False, True)
                    nc.scalar.copy(out=turned[u][:], in_=sums[u][:])
                    if u + BLOCKS < PE_UNITS:
                        sums.append(open_sum(u + BLOCKS))
                    back = psum.tile([P, HALF], F32, name=f"back{u}", tag=f"bank_a{u % BLOCKS}")
                    turn(back, turned[u][:], True, True)
                    nc.scalar.copy(out=res[j][:, cols], in_=back[:])
                    nc.scalar.dma_start(out=out_rows[j][:, cols], in_=res[j][:, cols])
                else:
                    nc.vector.tensor_tensor(res[j][:, cols], ya[j][:, cols], yb[j][:, cols], ADD)
                    nc.sync.dma_start(out=out_rows[j][:, cols], in_=res[j][:, cols])
